import numpy as np
import ml_dtypes


def mxq(x, axis, fmt="e4m3"):
    dtype, down = {"e4m3": (ml_dtypes.float8_e4m3fn, 7), "e5m2": (ml_dtypes.float8_e5m2, 14)}[fmt]
    v = np.moveaxis(np.asarray(x, np.float32).astype(ml_dtypes.bfloat16).astype(np.float64), axis, -1)
    blocks = v.reshape(v.shape[:-1] + (-1, 32))
    amax = np.abs(blocks).max(-1, keepdims=True)
    byte = np.maximum(np.where(amax > 0, np.frexp(amax)[1] - 1 + 127, 0) - down, 1)
    scale = np.exp2(byte - 127.0)
    codes = (blocks / scale).astype(np.float32).astype(dtype).astype(np.float64)
    return np.moveaxis((codes * scale).reshape(v.shape), -1, axis)


WIDE = False


def mx_kscale(k):
    if not WIDE:
        return np.ones(k)
    levels = np.array([10, -10, 5, -5, 0])
    if k % 512:
        return np.exp2(np.random.permutation(np.resize(levels, k // 32))).repeat(32)
    a = np.empty((k // 512, 16))
    for p in range(k // 512):
        a[p, :8] = np.random.permutation(np.resize(levels, 8))
        for g in range(8):
            far = levels[np.abs(levels - a[p, g]) >= 10]
            a[p, g + 8] = far[np.random.randint(len(far))]
    return np.exp2(a.ravel()).repeat(32)


BF16 = ml_dtypes.bfloat16


def bf(x):
    return np.asarray(x, np.float32).astype(BF16)


def f64(x):
    return np.asarray(x).astype(np.float64)


E2M1 = np.array([0.0, 0.5, 1.0, 1.5, 2.0, 3.0, 4.0, 6.0, -0.0, -0.5, -1.0, -1.5, -2.0, -3.0, -4.0, -6.0])


def pack_weight(w, fmt):
    k, n = w.shape
    w = f64(bf(w)).reshape(k // 32, 32, n)
    amax = np.abs(w).max(1)
    if fmt == "e4m3":
        byte = np.frexp(amax)[1] - 1 + 127 - 7
    else:
        mant, ex = np.frexp(amax / 6.0)
        byte = np.where(mant > 0.5, ex, ex - 1) + 127
    byte = np.clip(np.where(amax > 0, byte, 1), 1, 254)
    scaled = (w * np.exp2(127.0 - byte)[:, None, :]).reshape(k, n).astype(np.float32)
    by_word = np.ascontiguousarray(scaled.reshape(k // 512, 128, 4, n).transpose(0, 1, 3, 2))
    if fmt == "e4m3":
        words = by_word.astype(ml_dtypes.float8_e4m3fn).view(np.uint8)
    else:
        c = by_word.astype(ml_dtypes.float4_e2m1fn).view(np.uint8) & 0xF
        words = c[..., 0::2] | (c[..., 1::2] << 4)
    return np.ascontiguousarray(words), np.ascontiguousarray(byte.astype(np.uint8).reshape(k // 512, 16, n))


def unpack_weight(words, scales, fmt):
    g, p, n, _ = words.shape
    if fmt == "e4m3":
        vals = np.ascontiguousarray(words).view(ml_dtypes.float8_e4m3fn).astype(np.float64)
    else:
        nib = np.empty((g, p, n, 4), np.uint8)
        nib[..., 0::2] = words & 0xF
        nib[..., 1::2] = words >> 4
        vals = E2M1[nib]
    vals = vals * np.repeat(np.exp2(scales.astype(np.float64) - 127.0), 8, axis=1)[..., None]
    return vals.transpose(0, 1, 3, 2).reshape(g * 512, n)
def pack4(w):
    words, scales = pack_weight(w, "e2m1")
    return words.reshape(words.shape[0], 128, -1), scales


def unpack4(words, scales):
    return unpack_weight(words.reshape(words.shape[0], 128, -1, 2), scales, "e2m1")


A, M, K, N, L = 4, 512, 512, 1024, 512


def setup_inputs():
    s = mx_kscale(A * K)
    t = mx_kscale(A * N)
    cols = np.repeat(t.reshape(A, N), K, axis=0)
    g_words, g_scales = pack4(np.random.standard_normal((A * K, N)) / np.sqrt(K) / s[:, None] * cols)
    b_words, b_scales = pack4(np.random.standard_normal((A * K, N)) / np.sqrt(K) / s[:, None] * cols)
    h_words, h_scales = pack4(np.random.standard_normal((A * N, L)) / np.sqrt(N) / t[:, None])
    return {"src": bf(np.random.standard_normal((A, M, K)) * s.reshape(A, 1, K)),
            "vr": bf(1 + 0.5 * np.random.standard_normal((A, M, N))),
            "vi": bf(0.7 * np.random.standard_normal((A, M, N))),
            "g_words": g_words, "g_scales": g_scales,
            "b_words": b_words, "b_scales": b_scales,
            "h_words": h_words, "h_scales": h_scales}


def reference(src, vr, vi, g_words, g_scales, b_words, b_scales, h_words, h_scales):
    g = unpack4(g_words, g_scales).reshape(A, K, N)
    b = unpack4(b_words, b_scales).reshape(A, K, N)
    h = unpack4(h_words, h_scales).reshape(A, N, L)
    e = mxq(f64(src), 2, "e4m3")
    cr = e @ g
    ci = e @ b
    power = f64(vr) * cr + f64(vi) * ci
    return mxq(power, 2, "e4m3") @ h

@@ -1,0 +1,254 @@
+from contextlib import ExitStack
+
+import concourse.mybir as mybir
+from concourse.masks import make_identity
+
+A, M, K, N, L = 4, 512, 512, 1024, 512
+FLOPS = 2 * A * M * (2 * K * N + N * L)
+
+F32 = mybir.dt.float32
+BF16 = mybir.dt.bfloat16
+I32 = mybir.dt.int32
+U32 = mybir.dt.uint32
+U8 = mybir.dt.uint8
+FP8X4 = mybir.dt.float8_e4m3fn_x4
+FP4X4 = mybir.dt.float4_e2m1fn_x4
+MULT = mybir.AluOpType.mult
+ADD = mybir.AluOpType.add
+
+P = 128
+HALF = 512
+TILES = A * M // P
+PAIRS = TILES // 2
+
+
+def tile_split_real_ac_injections_s14_kernel(
+    tc, src, vr, vi, g_words, g_scales, b_words, b_scales, h_words, h_scales, out
+):
+    nc = tc.nc
+
+    def pair_rows(x, s):
+        a, h = divmod(s, 2)
+        return x[a, 256 * h : 256 * (h + 1), :].rearrange("(p j) c -> p j c", j=2)
+
+    with ExitStack() as ctx:
+        keep = ctx.enter_context(tc.tile_pool(name="keep", bufs=1))
+        work = ctx.enter_context(tc.tile_pool(name="work", bufs=3))
+        psum = ctx.enter_context(tc.psum_pool(name="psum", bufs=1))
+        ctx.enter_context(tc.manual_schedule())
+
+        ident = keep.tile([P, P], F32, name="ident")
+        make_identity(nc, ident[:])
+
+        def plane(name, groups, width):
+            t = keep.tile([P, groups, width], U8, name=name, align_bytes=64)
+            nc.vector.memset(t[:].bitcast(I32), 0)
+            return t
+
+        def load_plane(t, rows):
+            for r in range(4):
+                nc.sync.dma_start(
+                    out=t[:].bitcast(I32)[r:P:32, :, :],
+                    in_=rows[:, r:16:4, :].rearrange("g q n -> q g n").bitcast(I32),
+                )
+
+        def load(name, view, dtype):
+            t = keep.tile(list(view.shape), dtype, name=name, align_bytes=64)
+            nc.sync.dma_start(out=t[:], in_=view)
+            return t
+
+        def load_bytes(name, view):
+            t = keep.tile(list(view.shape), U8, name=name, align_bytes=64)
+            nc.sync.dma_start(out=t[:].bitcast(I32), in_=view.bitcast(I32))
+            return t
+
+        gs_first = plane("gs_first", 1, N)
+        bs_first = plane("bs_first", 1, N)
+        hs_all = plane("hs_all", 2 * A, L)
+        gs_rest = plane("gs_rest", A - 1, N)
+        bs_rest = plane("bs_rest", A - 1, N)
+
+        src_sb, volt, words, h_sb = {}, {}, {}, {}
+
+        def load_tile(kind, x, i):
+            return load("%s_t%d" % (kind, i), pair_rows(x, i // 2)[:, i % 2, :], BF16)[:]
+
+        def load_pair(kind, x, s):
+            t = load("%s_p%d" % (kind, s), pair_rows(x, s), BF16)
+            return [t[:, j, :] for j in range(2)]
+
+        def load_volt_pair(s):
+            for c, (kind, x) in enumerate((("vr", vr), ("vi", vi))):
+                volt[c, 2 * s], volt[c, 2 * s + 1] = load_pair(kind, x, s)
+
+        def load_h(a):
+            h_sb[a] = load_bytes("hw%d" % a, h_words[2 * a : 2 * a + 2].rearrange("g p n -> p g n"))
+
+        src_sb[0] = load_tile("src", src, 0)
+        src_sb[1] = load_tile("src", src, 1)
+        load_plane(gs_first, g_scales[0:1])
+        words[0, 0] = load_bytes("gw0", g_words[0])
+        volt[0, 0] = load_tile("vr", vr, 0)
+        words[1, 0] = load_bytes("bw0", b_words[0])
+        load_plane(bs_first, b_scales[0:1])
+        volt[1, 0] = load_tile("vi", vi, 0)
+        src_sb[2], src_sb[3] = load_pair("src", src, 1)
+        volt[0, 1] = load_tile("vr", vr, 1)
+        volt[1, 1] = load_tile("vi", vi, 1)
+        load_volt_pair(1)
+        src_sb[4], src_sb[5] = load_pair("src", src, 2)
+        load_plane(hs_all, h_scales)
+        load_plane(gs_rest, g_scales[1:A])
+        load_plane(bs_rest, b_scales[1:A])
+        load_h(0)
+        for s in range(2, PAIRS):
+            if s % 2 == 0:
+                a = s // 2
+                words[0, a] = load_bytes("gw%d" % a, g_words[a])
+                words[1, a] = load_bytes("bw%d" % a, b_words[a])
+            load_volt_pair(s)
+            if s + 1 < PAIRS:
+                src_sb[2 * s + 2], src_sb[2 * s + 3] = load_pair("src", src, s + 1)
+            if s % 2 == 0:
+                load_h(s // 2)
+
+        def weight_scales(c, a):
+            if a == 0:
+                return (gs_first, bs_first)[c][:, 0, :]
+            return (gs_rest, bs_rest)[c][:, a - 1, :]
+
+        src_q, power_q, current, prods, power, turned, q_in, flows = {}, {}, {}, {}, {}, {}, {}, {}
+
+        def turn(key, blocks):
+            bank = psum.tile([P, HALF], F32, name="turn", tag="turn", bufs=2)
+            for b, block in enumerate(blocks):
+                nc.tensor.transpose(bank[:, P * b : P * (b + 1)], block, ident[:])
+            turned[key] = bank[:, 0 : P * len(blocks)]
+
+        def turn_src(tiles):
+            turn(("src", tiles[0]), [src_sb[i].bitcast(F32)[:, u : K // 2 : 2] for i in tiles for u in range(2)])
+
+        def turn_power(i):
+            w = power[i][:].bitcast(F32)
+            turn(("power", i), [w[:, P * b : P * (b + 1)] for b in range(4)])
+
+        def interleave(key, dst):
+            nc.scalar.copy(
+                out=dst.bitcast(F32).rearrange("p (g m u) -> p g m u", m=P, u=2),
+                in_=turned[key].rearrange("p (g u m) -> p g m u", m=P, u=2),
+            )
+
+        def stage_inputs(step, power_tile, src_tiles):
+            width = (N if power_tile is not None else 0) + K * len(src_tiles)
+            t = work.tile([P, width], BF16, name="q_in", tag="q_in", align_bytes=64)
+            at = 0
+            if power_tile is not None:
+                interleave(("power", power_tile), t[:, 0:N])
+                at = N
+            if src_tiles:
+                interleave(("src", src_tiles[0]), t[:, at:width])
+            q_in[step] = (t, width, power_tile, src_tiles)
+
+        def quantize(step):
+            t, width, power_tile, src_tiles = q_in[step]
+            codes = work.tile([P, width // 4], U32, name="codes", tag="codes", bufs=5, align_bytes=64)
+            scales = work.tile([P, width // 4], U8, name="scales", tag="scales", bufs=5, align_bytes=64)
+            nc.vector.quantize_mx(out=codes[:].bitcast(FP8X4), scales=scales[:], in_=t[:])
+            at = 0
+            if power_tile is not None:
+                power_q[power_tile] = (codes, scales)
+                at = N // 4
+            for j, i in enumerate(src_tiles):
+                cols = slice(at + P * j, at + P * (j + 1))
+                src_q[i] = (codes[:, cols], scales[:, cols])
+
+        parts = [(c, g) for c in range(2) for g in range(2)]
+
+        def currents(i, c, g):
+            a = i // 4
+            bank = psum.tile([P, HALF], F32, name="cur", tag="cur%d%d" % (c, g))
+            codes, scales = src_q[i]
+            nc.tensor.matmul_mx(
+                out=bank[:],
+                lhsT=codes.bitcast(FP8X4),
+                lhsT_scale=scales,
+                rhs=words[c, a][:, 2 * HALF * g : 2 * HALF * (g + 1)].bitcast(FP4X4),
+                rhs_scale=weight_scales(c, a)[:, HALF * g : HALF * (g + 1)],
+                start=True,
+                stop=True,
+            )
+            current[i, c, g] = bank
+
+        def multiply(i, c, g):
+            if g == 0:
+                prods[i, c] = work.tile([P, N], F32, name="prod", tag="prod%d" % c)
+            cols = slice(HALF * g, HALF * (g + 1))
+            nc.vector.tensor_tensor(
+                out=prods[i, c][:, cols].rearrange("p (u q e) -> p u q e", u=2, e=2),
+                in0=current[i, c, g][:].rearrange("p (q u e) -> p u q e", u=2, e=2),
+                in1=volt[c, i][:, cols].rearrange("p (q u e) -> p u q e", u=2, e=2),
+                op=MULT,
+            )
+
+        def add_products(i, engine):
+            power[i] = work.tile([P, N], BF16, name="power", tag="power")
+            engine.tensor_tensor(out=power[i][:], in0=prods[i, 0][:], in1=prods[i, 1][:], op=ADD)
+
+        def line_flows(i):
+            a = i // 4
+            bank = psum.tile([P, L], F32, name="flow", tag="flow", bufs=2)
+            codes, scales = power_q[i]
+            for g in range(2):
+                nc.tensor.matmul_mx(
+                    out=bank[:],
+                    lhsT=codes[:, P * g : P * (g + 1)].bitcast(FP8X4),
+                    lhsT_scale=scales[:, P * g : P * (g + 1)],
+                    rhs=h_sb[a][:, g, :].bitcast(FP4X4),
+                    rhs_scale=hs_all[:, 2 * a + g, :],
+                    start=(g == 0),
+                    stop=(g == 1),
+                )
+            flows[i] = bank
+
+        def store(i):
+            res = keep.tile([P, L], F32, name="res%d" % i)
+            nc.scalar.copy(out=res[:], in_=flows[i][:])
+            nc.sync.dma_start(out=pair_rows(out, i // 2)[:, i % 2, :], in_=res[:])
+
+        def src_due(step):
+            s = step // 2 + 1
+            return [2 * s, 2 * s + 1] if step % 2 == 0 and 0 <= step and s < PAIRS else []
+
+        for i in range(2):
+            turn_src([i])
+        for i in range(2):
+            stage_inputs(("head", i), None, [i])
+            quantize(("head", i))
+        for c, g in parts:
+            currents(0, c, g)
+        turn_src(src_due(0))
+
+        for step in range(TILES + 3):
+            if step >= 3:
+                line_flows(step - 3)
+            quantised = step - 2 if 2 <= step < TILES + 2 else None
+            busy = quantised is not None or len(src_due(step)) > 0
+            if busy:
+                stage_inputs(step, quantised, src_due(step))
+            if step >= 3:
+                store(step - 3)
+            if step < TILES:
+                for c, g in parts:
+                    multiply(step, c, g)
+                    if step + 1 < TILES:
+                        currents(step + 1, c, g)
+                if step + 1 < TILES:
+                    add_products(step, nc.gpsimd)
+            if busy:
+                quantize(step)
+            if step == TILES - 1:
+                add_products(step, nc.vector)
+            if src_due(step + 1):
+                turn_src(src_due(step + 1))
+            if 1 <= step <= TILES:
+                turn_power(step - 1)

@@ -20,6 +20,8 @@ P = 128
 HALF = 512
 TILES = A * M // P
 PAIRS = TILES // 2
+VECTOR_SUM = 128
+GATE = 64
 
 
 def tile_split_real_ac_injections_s14_kernel(
@@ -128,9 +130,9 @@ def tile_split_real_ac_injections_s14_kernel(
         def turn_src(tiles):
             turn(("src", tiles[0]), [src_sb[i].bitcast(F32)[:, u : K // 2 : 2] for i in tiles for u in range(2)])
 
-        def turn_power(i):
+        def turn_power(i, halves=(0, 1)):
             w = power[i][:].bitcast(F32)
-            turn(("power", i), [w[:, P * b : P * (b + 1)] for b in range(4)])
+            turn(("power", i, halves[0]), [w[:, 256 * g + u : 256 * (g + 1) : 2] for g in halves for u in range(2)])
 
         def interleave(key, dst):
             nc.scalar.copy(
@@ -143,7 +145,7 @@ def tile_split_real_ac_injections_s14_kernel(
             t = work.tile([P, width], BF16, name="q_in", tag="q_in", align_bytes=64)
             at = 0
             if power_tile is not None:
-                interleave(("power", power_tile), t[:, 0:N])
+                interleave(("power", power_tile, 0), t[:, 0:N])
                 at = N
             if src_tiles:
                 interleave(("src", src_tiles[0]), t[:, at:width])
@@ -162,7 +164,7 @@ def tile_split_real_ac_injections_s14_kernel(
                 cols = slice(at + P * j, at + P * (j + 1))
                 src_q[i] = (codes[:, cols], scales[:, cols])
 
-        parts = [(c, g) for c in range(2) for g in range(2)]
+        parts = [(c, g) for g in range(2) for c in range(2)]
 
         def currents(i, c, g):
             a = i // 4
@@ -179,20 +181,18 @@ def tile_split_real_ac_injections_s14_kernel(
             )
             current[i, c, g] = bank
 
-        def multiply(i, c, g):
-            if g == 0:
+        def multiply(i, c, g, lo=0, hi=HALF):
+            if (i, c) not in prods:
                 prods[i, c] = work.tile([P, N], F32, name="prod", tag="prod%d" % c)
-            cols = slice(HALF * g, HALF * (g + 1))
+            cols = slice(HALF * g + lo, HALF * g + hi)
             nc.vector.tensor_tensor(
-                out=prods[i, c][:, cols].rearrange("p (u q e) -> p u q e", u=2, e=2),
-                in0=current[i, c, g][:].rearrange("p (q u e) -> p u q e", u=2, e=2),
-                in1=volt[c, i][:, cols].rearrange("p (q u e) -> p u q e", u=2, e=2),
-                op=MULT,
+                out=prods[i, c][:, cols], in0=current[i, c, g][:, lo:hi], in1=volt[c, i][:, cols], op=MULT
             )
 
-        def add_products(i, engine):
-            power[i] = work.tile([P, N], BF16, name="power", tag="power")
-            engine.tensor_tensor(out=power[i][:], in0=prods[i, 0][:], in1=prods[i, 1][:], op=ADD)
+        def add_products(i, engine, lo, hi):
+            if i not in power:
+                power[i] = work.tile([P, N], BF16, name="power", tag="power")
+            engine.tensor_tensor(out=power[i][:, lo:hi], in0=prods[i, 0][:, lo:hi], in1=prods[i, 1][:, lo:hi], op=ADD)
 
         def line_flows(i):
             a = i // 4
@@ -210,9 +210,12 @@ def tile_split_real_ac_injections_s14_kernel(
                 )
             flows[i] = bank
 
-        def store(i):
+        def store(i, on_vector=False):
             res = keep.tile([P, L], F32, name="res%d" % i)
-            nc.scalar.copy(out=res[:], in_=flows[i][:])
+            if on_vector:
+                nc.vector.tensor_copy(out=res[:], in_=flows[i][:])
+            else:
+                nc.scalar.copy(out=res[:], in_=flows[i][:])
             nc.sync.dma_start(out=pair_rows(out, i // 2)[:, i % 2, :], in_=res[:])
 
         def src_due(step):
@@ -228,27 +231,48 @@ def tile_split_real_ac_injections_s14_kernel(
             currents(0, c, g)
         turn_src(src_due(0))
 
-        for step in range(TILES + 3):
+        last = TILES - 1
+        for step in range(TILES):
             if step >= 3:
                 line_flows(step - 3)
-            quantised = step - 2 if 2 <= step < TILES + 2 else None
+            quantised = step - 2 if step >= 2 else None
             busy = quantised is not None or len(src_due(step)) > 0
             if busy:
                 stage_inputs(step, quantised, src_due(step))
             if step >= 3:
                 store(step - 3)
-            if step < TILES:
+            if step < last:
+                for c, g in parts[:3]:
+                    multiply(step, c, g)
+                    currents(step + 1, c, g)
+                multiply(step, 1, 1, 0, HALF - GATE)
+                add_products(step, nc.vector, 0, VECTOR_SUM)
+                multiply(step, 1, 1, HALF - GATE, HALF)
+                currents(step + 1, 1, 1)
+                add_products(step, nc.gpsimd, VECTOR_SUM, N)
+            else:
                 for c, g in parts:
                     multiply(step, c, g)
-                    if step + 1 < TILES:
-                        currents(step + 1, c, g)
-                if step + 1 < TILES:
-                    add_products(step, nc.gpsimd)
             if busy:
                 quantize(step)
-            if step == TILES - 1:
-                add_products(step, nc.vector)
             if src_due(step + 1):
                 turn_src(src_due(step + 1))
-            if 1 <= step <= TILES:
+            if step >= 1:
                 turn_power(step - 1)
+
+        line_flows(last - 2)
+        stage_inputs("before_last", last - 1, [])
+        final_in = work.tile([P, N], BF16, name="q_in", tag="q_in", align_bytes=64)
+        q_in["last"] = (final_in, N, last, [])
+        for g in range(2):
+            add_products(last, nc.vector, HALF * g, HALF * (g + 1))
+            turn_power(last, (g,))
+            if g == 0:
+                store(last - 2)
+            interleave(("power", last, g), final_in[:, HALF * g : HALF * (g + 1)])
+        quantize("before_last")
+        line_flows(last - 1)
+        quantize("last")
+        line_flows(last)
+        store(last - 1, True)
+        store(last)

@@ -186,7 +186,7 @@ def tile_split_real_ac_injections_s14_kernel(
                 prods[i, c] = work.tile([P, N], F32, name="prod", tag="prod%d" % c)
             cols = slice(HALF * g + lo, HALF * g + hi)
             nc.vector.tensor_tensor(
-                out=prods[i, c][:, cols], in0=current[i, c, g][:, lo:hi], in1=volt[c, i][:, cols], op=MULT
+                out=prods[i, c][:, cols], in0=volt[c, i][:, cols], in1=current[i, c, g][:, lo:hi], op=MULT
             )
 
         def add_products(i, engine, lo, hi):

@@ -19,9 +19,10 @@ ADD = mybir.AluOpType.add
 P = 128
 HALF = 512
 TILES = A * M // P
-PAIRS = TILES // 2
-VECTOR_SUM = 128
-GATE = 64
+TILES_PER_AREA = M // P
+TILE_PAIRS = TILES // 2
+VECTOR_SUM = 256
+GATE = 16
 
 
 def tile_split_real_ac_injections_s14_kernel(
@@ -31,7 +32,10 @@ def tile_split_real_ac_injections_s14_kernel(
 
     def pair_rows(x, s):
         a, h = divmod(s, 2)
-        return x[a, 256 * h : 256 * (h + 1), :].rearrange("(p j) c -> p j c", j=2)
+        return x[a, 2 * P * h : 2 * P * (h + 1), :].rearrange("(p j) c -> p j c", j=2)
+
+    def tile_rows(x, i):
+        return pair_rows(x, i // 2)[:, i % 2, :]
 
     with ExitStack() as ctx:
         keep = ctx.enter_context(tc.tile_pool(name="keep", bufs=1))
@@ -42,84 +46,110 @@ def tile_split_real_ac_injections_s14_kernel(
         ident = keep.tile([P, P], F32, name="ident")
         make_identity(nc, ident[:])
 
-        def plane(name, groups, width):
+
+        def scale_tile(name, groups, width):
             t = keep.tile([P, groups, width], U8, name=name, align_bytes=64)
             nc.vector.memset(t[:].bitcast(I32), 0)
             return t
 
-        def load_plane(t, rows):
+        def load_scales(t, rows):
             for r in range(4):
                 nc.sync.dma_start(
                     out=t[:].bitcast(I32)[r:P:32, :, :],
                     in_=rows[:, r:16:4, :].rearrange("g q n -> q g n").bitcast(I32),
                 )
 
-        def load(name, view, dtype):
-            t = keep.tile(list(view.shape), dtype, name=name, align_bytes=64)
+        def load(name, view):
+            t = keep.tile(list(view.shape), BF16, name=name, align_bytes=64)
             nc.sync.dma_start(out=t[:], in_=view)
             return t
 
-        def load_bytes(name, view):
+        def load_codes(name, view):
             t = keep.tile(list(view.shape), U8, name=name, align_bytes=64)
             nc.sync.dma_start(out=t[:].bitcast(I32), in_=view.bitcast(I32))
             return t
 
-        gs_first = plane("gs_first", 1, N)
-        bs_first = plane("bs_first", 1, N)
-        hs_all = plane("hs_all", 2 * A, L)
-        gs_rest = plane("gs_rest", A - 1, N)
-        bs_rest = plane("bs_rest", A - 1, N)
+        admittance_runs = ((0, 1), (1, 2), (2, A))
+        flow_runs = ((0, 1), (1, A))
+        admittance_scales = [
+            [scale_tile("%s_scales%d" % (kind, lo), hi - lo, N) for kind in ("g", "b")] for lo, hi in admittance_runs
+        ]
+        flow_scales = [scale_tile("h_scales%d" % lo, 2 * (hi - lo), L) for lo, hi in flow_runs]
 
-        src_sb, volt, words, h_sb = {}, {}, {}, {}
+        volt_in = (("vr", vr), ("vi", vi))
+        admittance_in = (("g", g_words, g_scales), ("b", b_words, b_scales))
+        src_tile, src_pair, volt, admittance, flow_factor = {}, {}, {}, {}, {}
 
-        def load_tile(kind, x, i):
-            return load("%s_t%d" % (kind, i), pair_rows(x, i // 2)[:, i % 2, :], BF16)[:]
+        def load_volt_tile(c, i):
+            kind, x = volt_in[c]
+            volt[c, i] = load("%s_tile%d" % (kind, i), tile_rows(x, i))[:]
 
-        def load_pair(kind, x, s):
-            t = load("%s_p%d" % (kind, s), pair_rows(x, s), BF16)
-            return [t[:, j, :] for j in range(2)]
+        def load_volt_tiles(tiles):
+            for i in tiles:
+                for c in range(2):
+                    load_volt_tile(c, i)
 
         def load_volt_pair(s):
-            for c, (kind, x) in enumerate((("vr", vr), ("vi", vi))):
-                volt[c, 2 * s], volt[c, 2 * s + 1] = load_pair(kind, x, s)
+            for c, (kind, x) in enumerate(volt_in):
+                t = load("%s_pair%d" % (kind, s), pair_rows(x, s))
+                volt[c, 2 * s], volt[c, 2 * s + 1] = t[:, 0, :], t[:, 1, :]
 
-        def load_h(a):
-            h_sb[a] = load_bytes("hw%d" % a, h_words[2 * a : 2 * a + 2].rearrange("g p n -> p g n"))
+        def load_src_pair(s):
+            src_pair[s] = load("src_pair%d" % s, pair_rows(src, s))
 
-        src_sb[0] = load_tile("src", src, 0)
-        src_sb[1] = load_tile("src", src, 1)
-        load_plane(gs_first, g_scales[0:1])
-        words[0, 0] = load_bytes("gw0", g_words[0])
-        volt[0, 0] = load_tile("vr", vr, 0)
-        words[1, 0] = load_bytes("bw0", b_words[0])
-        load_plane(bs_first, b_scales[0:1])
-        volt[1, 0] = load_tile("vi", vi, 0)
-        src_sb[2], src_sb[3] = load_pair("src", src, 1)
-        volt[0, 1] = load_tile("vr", vr, 1)
-        volt[1, 1] = load_tile("vi", vi, 1)
-        load_volt_pair(1)
-        src_sb[4], src_sb[5] = load_pair("src", src, 2)
-        load_plane(hs_all, h_scales)
-        load_plane(gs_rest, g_scales[1:A])
-        load_plane(bs_rest, b_scales[1:A])
-        load_h(0)
-        for s in range(2, PAIRS):
-            if s % 2 == 0:
-                a = s // 2
-                words[0, a] = load_bytes("gw%d" % a, g_words[a])
-                words[1, a] = load_bytes("bw%d" % a, b_words[a])
-            load_volt_pair(s)
-            if s + 1 < PAIRS:
-                src_sb[2 * s + 2], src_sb[2 * s + 3] = load_pair("src", src, s + 1)
-            if s % 2 == 0:
-                load_h(s // 2)
+        def load_admittance(c, a):
+            kind, codes_in, unused = admittance_in[c]
+            admittance[c, a] = load_codes("%s_codes%d" % (kind, a), codes_in[a])
 
-        def weight_scales(c, a):
-            if a == 0:
-                return (gs_first, bs_first)[c][:, 0, :]
-            return (gs_rest, bs_rest)[c][:, a - 1, :]
+        def load_admittance_scales(c, run):
+            lo, hi = admittance_runs[run]
+            load_scales(admittance_scales[run][c], admittance_in[c][2][lo:hi])
 
-        src_q, power_q, current, prods, power, turned, q_in, flows = {}, {}, {}, {}, {}, {}, {}, {}
+        def load_flow_scales(run):
+            lo, hi = flow_runs[run]
+            load_scales(flow_scales[run], h_scales[2 * lo : 2 * hi])
+
+        def load_flow_factor(a):
+            flow_factor[a] = load_codes("h_codes%d" % a, h_words[2 * a : 2 * a + 2].rearrange("g p n -> p g n"))
+
+        for i in range(2):
+            src_tile[i] = load("src_tile%d" % i, tile_rows(src, i))[:]
+        load_admittance_scales(0, 0)
+        load_admittance(0, 0)
+        load_volt_tile(0, 0)
+        load_admittance(1, 0)
+        load_admittance_scales(1, 0)
+        load_volt_tile(1, 0)
+        load_src_pair(1)
+        src_tile[2], src_tile[3] = src_pair[1][:, 0, :], src_pair[1][:, 1, :]
+        load_volt_tiles([1])
+        load_src_pair(2)
+        load_volt_tiles([2, 3])
+        load_admittance_scales(0, 1)
+        load_admittance_scales(1, 1)
+        load_flow_scales(0)
+        load_flow_factor(0)
+        load_admittance(0, 1)
+        load_admittance(1, 1)
+        load_src_pair(3)
+        load_volt_tiles([4, 5])
+        load_src_pair(4)
+        load_volt_pair(3)
+        load_admittance_scales(0, 2)
+        load_admittance_scales(1, 2)
+        load_flow_scales(1)
+        load_flow_factor(1)
+        for a in range(2, A):
+            load_admittance(0, a)
+            load_admittance(1, a)
+            for s in (2 * a, 2 * a + 1):
+                if s + 1 < TILE_PAIRS:
+                    load_src_pair(s + 1)
+                load_volt_pair(s)
+            load_flow_factor(a)
+
+
+        src_sorted, src_q, current, product, power, turned, staged, power_q, flow = ({} for stage in range(9))
 
         def turn(key, blocks):
             bank = psum.tile([P, HALF], F32, name="turn", tag="turn", bufs=2)
@@ -127,152 +157,165 @@ def tile_split_real_ac_injections_s14_kernel(
                 nc.tensor.transpose(bank[:, P * b : P * (b + 1)], block, ident[:])
             turned[key] = bank[:, 0 : P * len(blocks)]
 
-        def turn_src(tiles):
-            turn(("src", tiles[0]), [src_sb[i].bitcast(F32)[:, u : K // 2 : 2] for i in tiles for u in range(2)])
+        def turn_src_as_loaded(tiles):
+            turn(("src", tiles[0]), [src_tile[i].bitcast(F32)[:, u : K // 2 : 2] for i in tiles for u in range(2)])
 
-        def turn_power(i, halves=(0, 1)):
-            w = power[i][:].bitcast(F32)
-            turn(("power", i, halves[0]), [w[:, 256 * g + u : 256 * (g + 1) : 2] for g in halves for u in range(2)])
+        def sort_src(tiles):
+            t = work.tile([P, 2, 2, P], F32, name="src_sorted", tag="src_sorted", bufs=2)
+            nc.scalar.copy(out=t[:], in_=src_pair[tiles[0] // 2][:].bitcast(F32).rearrange("p j (q u) -> p j u q", u=2))
+            src_sorted[tiles[0]] = t
 
-        def interleave(key, dst):
-            nc.scalar.copy(
-                out=dst.bitcast(F32).rearrange("p (g m u) -> p g m u", m=P, u=2),
-                in_=turned[key].rearrange("p (g u m) -> p g m u", m=P, u=2),
-            )
+        def turn_sorted_src(tiles):
+            t = src_sorted[tiles[0]]
+            turn(("src", tiles[0]), [t[:, j, u, :] for j in range(2) for u in range(2)])
 
-        def stage_inputs(step, power_tile, src_tiles):
-            width = (N if power_tile is not None else 0) + K * len(src_tiles)
-            t = work.tile([P, width], BF16, name="q_in", tag="q_in", align_bytes=64)
-            at = 0
-            if power_tile is not None:
-                interleave(("power", power_tile, 0), t[:, 0:N])
-                at = N
-            if src_tiles:
-                interleave(("src", src_tiles[0]), t[:, at:width])
-            q_in[step] = (t, width, power_tile, src_tiles)
+        def turn_power(i, halves):
+            pairs = power[i][:].bitcast(F32)
+            blocks = [pairs[:, P * (2 * g + u) : P * (2 * g + u + 1)] for g in halves for u in range(2)]
+            turn(("power", i, halves[0]), blocks)
 
-        def quantize(step):
-            t, width, power_tile, src_tiles = q_in[step]
-            codes = work.tile([P, width // 4], U32, name="codes", tag="codes", bufs=5, align_bytes=64)
-            scales = work.tile([P, width // 4], U8, name="scales", tag="scales", bufs=5, align_bytes=64)
-            nc.vector.quantize_mx(out=codes[:].bitcast(FP8X4), scales=scales[:], in_=t[:])
-            at = 0
-            if power_tile is not None:
-                power_q[power_tile] = (codes, scales)
-                at = N // 4
-            for j, i in enumerate(src_tiles):
-                cols = slice(at + P * j, at + P * (j + 1))
-                src_q[i] = (codes[:, cols], scales[:, cols])
+        def stage(step, keys):
+            widths = [2 * turned[key].shape[1] for key in keys]
+            t = work.tile([P, sum(widths)], BF16, name="q_in", tag="q_in", align_bytes=64)
+            for n, key in enumerate(keys):
+                at = sum(widths[:n])
+                nc.scalar.copy(
+                    out=t[:, at : at + widths[n]].bitcast(F32).rearrange("p (g m u) -> p g m u", m=P, u=2),
+                    in_=turned[key].rearrange("p (g u m) -> p g m u", m=P, u=2),
+                )
+            staged[step] = t
+
+        def quantize(step, operands):
+            width = P * len(operands)
+            codes = work.tile([P, width], U32, name="codes", tag="codes", bufs=5, align_bytes=64)
+            scales = work.tile([P, width], U8, name="scales", tag="scales", bufs=5, align_bytes=64)
+            nc.vector.quantize_mx(out=codes[:].bitcast(FP8X4), scales=scales[:], in_=staged[step][:])
+            for n, (table, key) in enumerate(operands):
+                table[key] = (codes[:, P * n : P * (n + 1)], scales[:, P * n : P * (n + 1)])
 
         parts = [(c, g) for g in range(2) for c in range(2)]
 
         def currents(i, c, g):
-            a = i // 4
-            bank = psum.tile([P, HALF], F32, name="cur", tag="cur%d%d" % (c, g))
+            a = i // TILES_PER_AREA
+            run = min(a, len(admittance_runs) - 1)
+            bank = psum.tile([P, HALF], F32, name="current", tag="current%d%d" % (c, g))
             codes, scales = src_q[i]
             nc.tensor.matmul_mx(
                 out=bank[:],
                 lhsT=codes.bitcast(FP8X4),
                 lhsT_scale=scales,
-                rhs=words[c, a][:, 2 * HALF * g : 2 * HALF * (g + 1)].bitcast(FP4X4),
-                rhs_scale=weight_scales(c, a)[:, HALF * g : HALF * (g + 1)],
+                rhs=admittance[c, a][:, 2 * HALF * g : 2 * HALF * (g + 1)].bitcast(FP4X4),
+                rhs_scale=admittance_scales[run][c][:, a - admittance_runs[run][0], HALF * g : HALF * (g + 1)],
                 start=True,
                 stop=True,
             )
             current[i, c, g] = bank
 
-        def multiply(i, c, g, lo=0, hi=HALF):
-            if (i, c) not in prods:
-                prods[i, c] = work.tile([P, N], F32, name="prod", tag="prod%d" % c)
-            cols = slice(HALF * g + lo, HALF * g + hi)
+        def multiply(i, c, g, q_lo=0, q_hi=P):
+            if (i, c) not in product:
+                product[i, c] = work.tile([P, N], F32, name="product", tag="product%d" % c)
+            cols = slice(HALF * g, HALF * (g + 1))
             nc.vector.tensor_tensor(
-                out=prods[i, c][:, cols], in0=volt[c, i][:, cols], in1=current[i, c, g][:, lo:hi], op=MULT
+                out=product[i, c][:, cols].rearrange("p (u q e) -> p u q e", u=2, e=2)[:, :, q_lo:q_hi, :],
+                in0=volt[c, i][:, cols].rearrange("p (q u e) -> p u q e", u=2, e=2)[:, :, q_lo:q_hi, :],
+                in1=current[i, c, g][:].rearrange("p (q u e) -> p u q e", u=2, e=2)[:, :, q_lo:q_hi, :],
+                op=MULT,
             )
 
         def add_products(i, engine, lo, hi):
             if i not in power:
                 power[i] = work.tile([P, N], BF16, name="power", tag="power")
-            engine.tensor_tensor(out=power[i][:, lo:hi], in0=prods[i, 0][:, lo:hi], in1=prods[i, 1][:, lo:hi], op=ADD)
+            engine.tensor_tensor(
+                out=power[i][:, lo:hi], in0=product[i, 0][:, lo:hi], in1=product[i, 1][:, lo:hi], op=ADD
+            )
 
-        def line_flows(i):
-            a = i // 4
-            bank = psum.tile([P, L], F32, name="flow", tag="flow", bufs=2)
-            codes, scales = power_q[i]
-            for g in range(2):
+        def line_flows(i, halves):
+            a = i // TILES_PER_AREA
+            run = min(a, len(flow_runs) - 1)
+            if i not in flow:
+                flow[i] = psum.tile([P, L], F32, name="flow", tag="flow", bufs=2)
+            for g in halves:
+                codes, scales = power_q[i, g]
                 nc.tensor.matmul_mx(
-                    out=bank[:],
-                    lhsT=codes[:, P * g : P * (g + 1)].bitcast(FP8X4),
-                    lhsT_scale=scales[:, P * g : P * (g + 1)],
-                    rhs=h_sb[a][:, g, :].bitcast(FP4X4),
-                    rhs_scale=hs_all[:, 2 * a + g, :],
+                    out=flow[i][:],
+                    lhsT=codes.bitcast(FP8X4),
+                    lhsT_scale=scales,
+                    rhs=flow_factor[a][:, g, :].bitcast(FP4X4),
+                    rhs_scale=flow_scales[run][:, 2 * (a - flow_runs[run][0]) + g, :],
                     start=(g == 0),
                     stop=(g == 1),
                 )
-            flows[i] = bank
 
-        def store(i, on_vector=False):
-            res = keep.tile([P, L], F32, name="res%d" % i)
-            if on_vector:
-                nc.vector.tensor_copy(out=res[:], in_=flows[i][:])
-            else:
-                nc.scalar.copy(out=res[:], in_=flows[i][:])
-            nc.sync.dma_start(out=pair_rows(out, i // 2)[:, i % 2, :], in_=res[:])
+        def store(i, copy):
+            result = keep.tile([P, L], F32, name="result%d" % i)
+            copy(out=result[:], in_=flow[i][:])
+            nc.sync.dma_start(out=tile_rows(out, i), in_=result[:])
 
         def src_due(step):
-            s = step // 2 + 1
-            return [2 * s, 2 * s + 1] if step % 2 == 0 and 0 <= step and s < PAIRS else []
+            return [step + 2, step + 3] if step % 2 == 0 and step + 2 < TILES else []
+
+        both = (0, 1)
+        last = TILES - 1
 
         for i in range(2):
-            turn_src([i])
+            turn_src_as_loaded([i])
         for i in range(2):
-            stage_inputs(("head", i), None, [i])
-            quantize(("head", i))
+            stage(("head", i), [("src", i)])
+            quantize(("head", i), [(src_q, i)])
         for c, g in parts:
             currents(0, c, g)
-        turn_src(src_due(0))
+        turn_src_as_loaded(src_due(0))
 
-        last = TILES - 1
         for step in range(TILES):
+            keys, operands = [], []
+            if step >= 2:
+                keys.append(("power", step - 2, 0))
+                operands.extend([(power_q, (step - 2, g)) for g in both])
+            if src_due(step):
+                keys.append(("src", src_due(step)[0]))
+                operands.extend([(src_q, i) for i in src_due(step)])
+
             if step >= 3:
-                line_flows(step - 3)
-            quantised = step - 2 if step >= 2 else None
-            busy = quantised is not None or len(src_due(step)) > 0
-            if busy:
-                stage_inputs(step, quantised, src_due(step))
+                line_flows(step - 3, both)
+            if keys:
+                stage(step, keys)
             if step >= 3:
-                store(step - 3)
-            if step < last:
-                for c, g in parts[:3]:
-                    multiply(step, c, g)
+                store(step - 3, nc.scalar.copy)
+            if src_due(step + 1):
+                sort_src(src_due(step + 1))
+            for c, g in parts[:3]:
+                multiply(step, c, g)
+                if step < last:
                     currents(step + 1, c, g)
-                multiply(step, 1, 1, 0, HALF - GATE)
+            if src_due(step + 1):
+                turn_sorted_src(src_due(step + 1))
+            if step >= 1:
+                turn_power(step - 1, both)
+            if step < last:
+                multiply(step, 1, 1, 0, P - GATE)
                 add_products(step, nc.vector, 0, VECTOR_SUM)
-                multiply(step, 1, 1, HALF - GATE, HALF)
+                if keys:
+                    quantize(step, operands)
+                multiply(step, 1, 1, P - GATE, P)
                 currents(step + 1, 1, 1)
                 add_products(step, nc.gpsimd, VECTOR_SUM, N)
             else:
-                for c, g in parts:
-                    multiply(step, c, g)
-            if busy:
-                quantize(step)
-            if src_due(step + 1):
-                turn_src(src_due(step + 1))
-            if step >= 1:
-                turn_power(step - 1)
+                multiply(step, 1, 1)
+                quantize(step, operands)
 
-        line_flows(last - 2)
-        stage_inputs("before_last", last - 1, [])
-        final_in = work.tile([P, N], BF16, name="q_in", tag="q_in", align_bytes=64)
-        q_in["last"] = (final_in, N, last, [])
-        for g in range(2):
-            add_products(last, nc.vector, HALF * g, HALF * (g + 1))
-            turn_power(last, (g,))
-            if g == 0:
-                store(last - 2)
-            interleave(("power", last, g), final_in[:, HALF * g : HALF * (g + 1)])
-        quantize("before_last")
-        line_flows(last - 1)
-        quantize("last")
-        line_flows(last)
-        store(last - 1, True)
-        store(last)
+        line_flows(last - 2, both)
+        stage("before last", [("power", last - 1, 0)])
+        add_products(last, nc.vector, 0, HALF)
+        turn_power(last, (0,))
+        store(last - 2, nc.scalar.copy)
+        stage(("last", 0), [("power", last, 0)])
+        add_products(last, nc.vector, HALF, N)
+        turn_power(last, (1,))
+        quantize("before last", [(power_q, (last - 1, g)) for g in both])
+        line_flows(last - 1, both)
+        stage(("last", 1), [("power", last, 1)])
+        for g in both:
+            quantize(("last", g), [(power_q, (last, g))])
+            line_flows(last, (g,))
+        store(last - 1, nc.vector.tensor_copy)
+        store(last, nc.scalar.copy)

@@ -21,7 +21,7 @@ HALF = 512
 TILES = A * M // P
 TILES_PER_AREA = M // P
 TILE_PAIRS = TILES // 2
-VECTOR_SUM = 256
+EARLY_SUM = N - HALF - HALF // 2
 GATE = 16
 
 
@@ -125,16 +125,18 @@ def tile_split_real_ac_injections_s14_kernel(
         load_volt_tiles([1])
         load_src_pair(2)
         load_volt_tiles([2, 3])
+        load_src_pair(3)
         load_admittance_scales(0, 1)
         load_admittance_scales(1, 1)
         load_flow_scales(0)
         load_flow_factor(0)
         load_admittance(0, 1)
         load_admittance(1, 1)
-        load_src_pair(3)
-        load_volt_tiles([4, 5])
+        load_volt_tiles([4])
         load_src_pair(4)
+        load_volt_tiles([5])
         load_volt_pair(3)
+        load_src_pair(5)
         load_admittance_scales(0, 2)
         load_admittance_scales(1, 2)
         load_flow_scales(1)
@@ -143,9 +145,9 @@ def tile_split_real_ac_injections_s14_kernel(
             load_admittance(0, a)
             load_admittance(1, a)
             for s in (2 * a, 2 * a + 1):
-                if s + 1 < TILE_PAIRS:
-                    load_src_pair(s + 1)
                 load_volt_pair(s)
+                if s + 2 < TILE_PAIRS:
+                    load_src_pair(s + 2)
             load_flow_factor(a)
 
 
@@ -158,7 +160,7 @@ def tile_split_real_ac_injections_s14_kernel(
             turned[key] = bank[:, 0 : P * len(blocks)]
 
         def turn_src_as_loaded(tiles):
-            turn(("src", tiles[0]), [src_tile[i].bitcast(F32)[:, u : K // 2 : 2] for i in tiles for u in range(2)])
+            turn(("src", tiles[0], len(tiles)), [src_tile[i].bitcast(F32)[:, u : K // 2 : 2] for i in tiles for u in range(2)])
 
         def sort_src(tiles):
             t = work.tile([P, 2, 2, P], F32, name="src_sorted", tag="src_sorted", bufs=2)
@@ -167,23 +169,43 @@ def tile_split_real_ac_injections_s14_kernel(
 
         def turn_sorted_src(tiles):
             t = src_sorted[tiles[0]]
-            turn(("src", tiles[0]), [t[:, j, u, :] for j in range(2) for u in range(2)])
+            turn(("src", tiles[0], 2), [t[:, j, u, :] for j in range(2) for u in range(2)])
 
         def turn_power(i, halves):
             pairs = power[i][:].bitcast(F32)
             blocks = [pairs[:, P * (2 * g + u) : P * (2 * g + u + 1)] for g in halves for u in range(2)]
-            turn(("power", i, halves[0]), blocks)
+            turn(("power", i, len(halves)), blocks)
 
-        def stage(step, keys):
-            widths = [2 * turned[key].shape[1] for key in keys]
-            t = work.tile([P, sum(widths)], BF16, name="q_in", tag="q_in", align_bytes=64)
-            for n, key in enumerate(keys):
-                at = sum(widths[:n])
+        def turn_and_add(i):
+            bank = psum.tile([P, HALF], F32, name="turn", tag="turn", bufs=2)
+            for t in range(4):
+                cols = slice(P * t, P * (t + 1))
+                for c in range(2):
+                    nc.tensor.matmul(
+                        out=bank[:, cols],
+                        lhsT=product[i, c][:, cols],
+                        rhs=ident[:],
+                        is_transpose=True,
+                        start=(c == 0),
+                        stop=(c == 1),
+                    )
+            turned["sum", i, 1] = bank[:]
+
+        def stage(step, keys, key):
+            widths = [HALF * passes for name, tile, passes in keys]
+            if step not in staged:
+                staged[step] = work.tile([P, sum(widths)], BF16, name="q_in", tag="q_in", align_bytes=64)
+            n = keys.index(key)
+            dst = staged[step][:, sum(widths[:n]) : sum(widths[: n + 1])]
+            if key[0] == "sum":
                 nc.scalar.copy(
-                    out=t[:, at : at + widths[n]].bitcast(F32).rearrange("p (g m u) -> p g m u", m=P, u=2),
+                    out=dst.rearrange("p (m t) -> p m t", t=4), in_=turned[key].rearrange("p (t m) -> p m t", t=4)
+                )
+            else:
+                nc.scalar.copy(
+                    out=dst.bitcast(F32).rearrange("p (g m u) -> p g m u", m=P, u=2),
                     in_=turned[key].rearrange("p (g u m) -> p g m u", m=P, u=2),
                 )
-            staged[step] = t
 
         def quantize(step, operands):
             width = P * len(operands)
@@ -215,12 +237,16 @@ def tile_split_real_ac_injections_s14_kernel(
             if (i, c) not in product:
                 product[i, c] = work.tile([P, N], F32, name="product", tag="product%d" % c)
             cols = slice(HALF * g, HALF * (g + 1))
-            nc.vector.tensor_tensor(
-                out=product[i, c][:, cols].rearrange("p (u q e) -> p u q e", u=2, e=2)[:, :, q_lo:q_hi, :],
-                in0=volt[c, i][:, cols].rearrange("p (q u e) -> p u q e", u=2, e=2)[:, :, q_lo:q_hi, :],
-                in1=current[i, c, g][:].rearrange("p (q u e) -> p u q e", u=2, e=2)[:, :, q_lo:q_hi, :],
-                op=MULT,
-            )
+            if i % 2 == 1 and g == 0:
+                dst = product[i, c][:, cols].rearrange("p (t q) -> p t q", t=4)
+                factors = [x.rearrange("p (q t) -> p t q", t=4) for x in (volt[c, i][:, cols], current[i, c, g][:])]
+            else:
+                dst = product[i, c][:, cols].rearrange("p (u q e) -> p u q e", u=2, e=2)[:, :, q_lo:q_hi, :]
+                factors = [
+                    x.rearrange("p (q u e) -> p u q e", u=2, e=2)[:, :, q_lo:q_hi, :]
+                    for x in (volt[c, i][:, cols], current[i, c, g][:])
+                ]
+            nc.vector.tensor_tensor(out=dst, in0=factors[0], in1=factors[1], op=MULT)
 
         def add_products(i, engine, lo, hi):
             if i not in power:
@@ -233,7 +259,10 @@ def tile_split_real_ac_injections_s14_kernel(
             a = i // TILES_PER_AREA
             run = min(a, len(flow_runs) - 1)
             if i not in flow:
-                flow[i] = psum.tile([P, L], F32, name="flow", tag="flow", bufs=2)
+                if i == TILES - 1:
+                    flow[i] = psum.tile([P, L], F32, name="last_flow", tag="current00")
+                else:
+                    flow[i] = psum.tile([P, L], F32, name="flow", tag="flow", bufs=2)
             for g in halves:
                 codes, scales = power_q[i, g]
                 nc.tensor.matmul_mx(
@@ -254,68 +283,82 @@ def tile_split_real_ac_injections_s14_kernel(
         def src_due(step):
             return [step + 2, step + 3] if step % 2 == 0 and step + 2 < TILES else []
 
+        def step_keys(step):
+            i = step - 2
+            keys = []
+            if i >= 0:
+                keys.extend([("sum", i, 1), ("power", i, 1)] if i % 2 == 1 else [("power", i, 2)])
+            if src_due(step):
+                keys.append(("src", src_due(step)[0], 2))
+            return keys
+
+        def step_operands(step):
+            operands = [(power_q, (step - 2, g)) for g in both] if step >= 2 else []
+            return operands + [(src_q, i) for i in src_due(step)]
+
         both = (0, 1)
         last = TILES - 1
 
         for i in range(2):
             turn_src_as_loaded([i])
         for i in range(2):
-            stage(("head", i), [("src", i)])
+            stage(("head", i), [("src", i, 1)], ("src", i, 1))
             quantize(("head", i), [(src_q, i)])
         for c, g in parts:
             currents(0, c, g)
         turn_src_as_loaded(src_due(0))
+        stage(0, step_keys(0), ("src", 2, 2))
 
         for step in range(TILES):
-            keys, operands = [], []
+            even = step % 2 == 0
             if step >= 2:
-                keys.append(("power", step - 2, 0))
-                operands.extend([(power_q, (step - 2, g)) for g in both])
-            if src_due(step):
-                keys.append(("src", src_due(step)[0]))
-                operands.extend([(src_q, i) for i in src_due(step)])
-
-            if step >= 3:
-                line_flows(step - 3, both)
-            if keys:
-                stage(step, keys)
-            if step >= 3:
-                store(step - 3, nc.scalar.copy)
-            if src_due(step + 1):
-                sort_src(src_due(step + 1))
-            for c, g in parts[:3]:
+                stage(step, step_keys(step), ("power", step - 2, 2 if even else 1))
+            if even and step >= 2:
+                stage(step + 1, step_keys(step + 1), ("sum", step - 1, 1))
+            if not even and src_due(step + 1):
+                stage(step + 1, step_keys(step + 1), ("src", src_due(step + 1)[0], 2))
+            if src_due(step + 2):
+                sort_src(src_due(step + 2))
+            for n, (c, g) in enumerate(parts[:3]):
                 multiply(step, c, g)
+                if n == 1 and step >= 3:
+                    line_flows(step - 3, both)
+                    store(step - 3, nc.scalar.copy)
                 if step < last:
                     currents(step + 1, c, g)
-            if src_due(step + 1):
-                turn_sorted_src(src_due(step + 1))
+            if even:
+                add_products(step, nc.gpsimd, 0, EARLY_SUM)
+            if step == last:
+                turn_and_add(step)
             if step >= 1:
-                turn_power(step - 1, both)
+                turn_power(step - 1, (1,) if even else both)
+            if src_due(step + 2):
+                turn_sorted_src(src_due(step + 2))
             if step < last:
+                if not even:
+                    turn_and_add(step)
                 multiply(step, 1, 1, 0, P - GATE)
-                add_products(step, nc.vector, 0, VECTOR_SUM)
-                if keys:
-                    quantize(step, operands)
+                if step_keys(step):
+                    quantize(step, step_operands(step))
                 multiply(step, 1, 1, P - GATE, P)
                 currents(step + 1, 1, 1)
-                add_products(step, nc.gpsimd, VECTOR_SUM, N)
+                add_products(step, nc.gpsimd, EARLY_SUM if even else HALF, N)
             else:
                 multiply(step, 1, 1)
-                quantize(step, operands)
+                quantize(step, step_operands(step))
 
+        stage(("last", 0), [("sum", last, 1)], ("sum", last, 1))
+        stage(TILES, step_keys(TILES), ("power", last - 1, 2))
         line_flows(last - 2, both)
-        stage("before last", [("power", last - 1, 0)])
-        add_products(last, nc.vector, 0, HALF)
-        turn_power(last, (0,))
-        store(last - 2, nc.scalar.copy)
-        stage(("last", 0), [("power", last, 0)])
         add_products(last, nc.vector, HALF, N)
         turn_power(last, (1,))
-        quantize("before last", [(power_q, (last - 1, g)) for g in both])
+        quantize(TILES, step_operands(TILES))
         line_flows(last - 1, both)
-        stage(("last", 1), [("power", last, 1)])
-        for g in both:
-            quantize(("last", g), [(power_q, (last, g))])
-            line_flows(last, (g,))
+        quantize(("last", 0), [(power_q, (last, 0))])
+        line_flows(last, (0,))
+        stage(("last", 1), [("power", last, 1)], ("power", last, 1))
+        store(last - 2, nc.scalar.copy)
+        quantize(("last", 1), [(power_q, (last, 1))])
+        line_flows(last, (1,))
         store(last - 1, nc.vector.tensor_copy)
         store(last, nc.scalar.copy)

from contextlib import ExitStack

import concourse.mybir as mybir
from concourse.masks import make_identity

A, M, K, N, L = 4, 512, 512, 1024, 512
FLOPS = 2 * A * M * (2 * K * N + N * L)

F32 = mybir.dt.float32
BF16 = mybir.dt.bfloat16
I32 = mybir.dt.int32
U32 = mybir.dt.uint32
U8 = mybir.dt.uint8
FP8X4 = mybir.dt.float8_e4m3fn_x4
FP4X4 = mybir.dt.float4_e2m1fn_x4
MULT = mybir.AluOpType.mult
ADD = mybir.AluOpType.add

P = 128
HALF = 512
TILES = A * M // P
TILES_PER_AREA = M // P
TILE_PAIRS = TILES // 2
EARLY_SUM = N - HALF - HALF // 2
GATE = 16


def tile_split_real_ac_injections_s14_kernel(
    tc, src, vr, vi, g_words, g_scales, b_words, b_scales, h_words, h_scales, out
):
    nc = tc.nc

    def pair_rows(x, s):
        a, h = divmod(s, 2)
        return x[a, 2 * P * h : 2 * P * (h + 1), :].rearrange("(p j) c -> p j c", j=2)

    def tile_rows(x, i):
        return pair_rows(x, i // 2)[:, i % 2, :]

    with ExitStack() as ctx:
        keep = ctx.enter_context(tc.tile_pool(name="keep", bufs=1))
        work = ctx.enter_context(tc.tile_pool(name="work", bufs=3))
        psum = ctx.enter_context(tc.psum_pool(name="psum", bufs=1))
        ctx.enter_context(tc.manual_schedule())

        ident = keep.tile([P, P], F32, name="ident")
        make_identity(nc, ident[:])


        def scale_tile(name, groups, width):
            t = keep.tile([P, groups, width], U8, name=name, align_bytes=64)
            nc.vector.memset(t[:].bitcast(I32), 0)
            return t

        def load_scales(t, rows):
            for r in range(4):
                nc.sync.dma_start(
                    out=t[:].bitcast(I32)[r:P:32, :, :],
                    in_=rows[:, r:16:4, :].rearrange("g q n -> q g n").bitcast(I32),
                )

        def load(name, view):
            t = keep.tile(list(view.shape), BF16, name=name, align_bytes=64)
            nc.sync.dma_start(out=t[:], in_=view)
            return t

        def load_codes(name, view):
            t = keep.tile(list(view.shape), U8, name=name, align_bytes=64)
            nc.sync.dma_start(out=t[:].bitcast(I32), in_=view.bitcast(I32))
            return t

        admittance_runs = ((0, 1), (1, 2), (2, A))
        flow_runs = ((0, 1), (1, A))
        admittance_scales = [
            [scale_tile("%s_scales%d" % (kind, lo), hi - lo, N) for kind in ("g", "b")] for lo, hi in admittance_runs
        ]
        flow_scales = [scale_tile("h_scales%d" % lo, 2 * (hi - lo), L) for lo, hi in flow_runs]

        volt_in = (("vr", vr), ("vi", vi))
        admittance_in = (("g", g_words, g_scales), ("b", b_words, b_scales))
        src_tile, src_pair, volt, admittance, flow_factor = {}, {}, {}, {}, {}

        def load_volt_tile(c, i):
            kind, x = volt_in[c]
            volt[c, i] = load("%s_tile%d" % (kind, i), tile_rows(x, i))[:]

        def load_volt_tiles(tiles):
            for i in tiles:
                for c in range(2):
                    load_volt_tile(c, i)

        def load_volt_pair(s):
            for c, (kind, x) in enumerate(volt_in):
                t = load("%s_pair%d" % (kind, s), pair_rows(x, s))
                volt[c, 2 * s], volt[c, 2 * s + 1] = t[:, 0, :], t[:, 1, :]

        def load_src_pair(s):
            src_pair[s] = load("src_pair%d" % s, pair_rows(src, s))

        def load_admittance(c, a):
            kind, codes_in, unused = admittance_in[c]
            admittance[c, a] = load_codes("%s_codes%d" % (kind, a), codes_in[a])

        def load_admittance_scales(c, run):
            lo, hi = admittance_runs[run]
            load_scales(admittance_scales[run][c], admittance_in[c][2][lo:hi])

        def load_flow_scales(run):
            lo, hi = flow_runs[run]
            load_scales(flow_scales[run], h_scales[2 * lo : 2 * hi])

        def load_flow_factor(a):
            flow_factor[a] = load_codes("h_codes%d" % a, h_words[2 * a : 2 * a + 2].rearrange("g p n -> p g n"))

        for i in range(2):
            src_tile[i] = load("src_tile%d" % i, tile_rows(src, i))[:]
        load_admittance_scales(0, 0)
        load_admittance(0, 0)
        load_volt_tile(0, 0)
        load_admittance(1, 0)
        load_admittance_scales(1, 0)
        load_volt_tile(1, 0)
        load_src_pair(1)
        src_tile[2], src_tile[3] = src_pair[1][:, 0, :], src_pair[1][:, 1, :]
        load_volt_tiles([1])
        load_src_pair(2)
        load_volt_tiles([2, 3])
        load_src_pair(3)
        load_admittance_scales(0, 1)
        load_admittance_scales(1, 1)
        load_flow_scales(0)
        load_flow_factor(0)
        load_admittance(0, 1)
        load_admittance(1, 1)
        load_volt_tiles([4])
        load_src_pair(4)
        load_volt_tiles([5])
        load_volt_pair(3)
        load_src_pair(5)
        load_admittance_scales(0, 2)
        load_admittance_scales(1, 2)
        load_flow_scales(1)
        load_flow_factor(1)
        for a in range(2, A):
            load_admittance(0, a)
            load_admittance(1, a)
            for s in (2 * a, 2 * a + 1):
                load_volt_pair(s)
                if s + 2 < TILE_PAIRS:
                    load_src_pair(s + 2)
            load_flow_factor(a)


        src_sorted, src_q, current, product, power, turned, staged, power_q, flow = ({} for stage in range(9))

        def turn(key, blocks):
            bank = psum.tile([P, HALF], F32, name="turn", tag="turn", bufs=2)
            for b, block in enumerate(blocks):
                nc.tensor.transpose(bank[:, P * b : P * (b + 1)], block, ident[:])
            turned[key] = bank[:, 0 : P * len(blocks)]

        def turn_src_as_loaded(tiles):
            turn(("src", tiles[0], len(tiles)), [src_tile[i].bitcast(F32)[:, u : K // 2 : 2] for i in tiles for u in range(2)])

        def sort_src(tiles):
            t = work.tile([P, 2, 2, P], F32, name="src_sorted", tag="src_sorted", bufs=2)
            nc.scalar.copy(out=t[:], in_=src_pair[tiles[0] // 2][:].bitcast(F32).rearrange("p j (q u) -> p j u q", u=2))
            src_sorted[tiles[0]] = t

        def turn_sorted_src(tiles):
            t = src_sorted[tiles[0]]
            turn(("src", tiles[0], 2), [t[:, j, u, :] for j in range(2) for u in range(2)])

        def turn_power(i, halves):
            pairs = power[i][:].bitcast(F32)
            blocks = [pairs[:, P * (2 * g + u) : P * (2 * g + u + 1)] for g in halves for u in range(2)]
            turn(("power", i, len(halves)), blocks)

        def turn_and_add(i):
            bank = psum.tile([P, HALF], F32, name="turn", tag="turn", bufs=2)
            for t in range(4):
                cols = slice(P * t, P * (t + 1))
                for c in range(2):
                    nc.tensor.matmul(
                        out=bank[:, cols],
                        lhsT=product[i, c][:, cols],
                        rhs=ident[:],
                        is_transpose=True,
                        start=(c == 0),
                        stop=(c == 1),
                    )
            turned["sum", i, 1] = bank[:]

        def stage(step, keys, key):
            widths = [HALF * passes for name, tile, passes in keys]
            if step not in staged:
                staged[step] = work.tile([P, sum(widths)], BF16, name="q_in", tag="q_in", align_bytes=64)
            n = keys.index(key)
            dst = staged[step][:, sum(widths[:n]) : sum(widths[: n + 1])]
            if key[0] == "sum":
                nc.scalar.copy(
                    out=dst.rearrange("p (m t) -> p m t", t=4), in_=turned[key].rearrange("p (t m) -> p m t", t=4)
                )
            else:
                nc.scalar.copy(
                    out=dst.bitcast(F32).rearrange("p (g m u) -> p g m u", m=P, u=2),
                    in_=turned[key].rearrange("p (g u m) -> p g m u", m=P, u=2),
                )

        def quantize(step, operands):
            width = P * len(operands)
            codes = work.tile([P, width], U32, name="codes", tag="codes", bufs=5, align_bytes=64)
            scales = work.tile([P, width], U8, name="scales", tag="scales", bufs=5, align_bytes=64)
            nc.vector.quantize_mx(out=codes[:].bitcast(FP8X4), scales=scales[:], in_=staged[step][:])
            for n, (table, key) in enumerate(operands):
                table[key] = (codes[:, P * n : P * (n + 1)], scales[:, P * n : P * (n + 1)])

        parts = [(c, g) for g in range(2) for c in range(2)]

        def currents(i, c, g):
            a = i // TILES_PER_AREA
            run = min(a, len(admittance_runs) - 1)
            bank = psum.tile([P, HALF], F32, name="current", tag="current%d%d" % (c, g))
            codes, scales = src_q[i]
            nc.tensor.matmul_mx(
                out=bank[:],
                lhsT=codes.bitcast(FP8X4),
                lhsT_scale=scales,
                rhs=admittance[c, a][:, 2 * HALF * g : 2 * HALF * (g + 1)].bitcast(FP4X4),
                rhs_scale=admittance_scales[run][c][:, a - admittance_runs[run][0], HALF * g : HALF * (g + 1)],
                start=True,
                stop=True,
            )
            current[i, c, g] = bank

        def multiply(i, c, g, q_lo=0, q_hi=P):
            if (i, c) not in product:
                product[i, c] = work.tile([P, N], F32, name="product", tag="product%d" % c)
            cols = slice(HALF * g, HALF * (g + 1))
            if i % 2 == 1 and g == 0:
                dst = product[i, c][:, cols].rearrange("p (t q) -> p t q", t=4)
                factors = [x.rearrange("p (q t) -> p t q", t=4) for x in (volt[c, i][:, cols], current[i, c, g][:])]
            else:
                dst = product[i, c][:, cols].rearrange("p (u q e) -> p u q e", u=2, e=2)[:, :, q_lo:q_hi, :]
                factors = [
                    x.rearrange("p (q u e) -> p u q e", u=2, e=2)[:, :, q_lo:q_hi, :]
                    for x in (volt[c, i][:, cols], current[i, c, g][:])
                ]
            nc.vector.tensor_tensor(out=dst, in0=factors[0], in1=factors[1], op=MULT)

        def add_products(i, engine, lo, hi):
            if i not in power:
                power[i] = work.tile([P, N], BF16, name="power", tag="power")
            engine.tensor_tensor(
                out=power[i][:, lo:hi], in0=product[i, 0][:, lo:hi], in1=product[i, 1][:, lo:hi], op=ADD
            )

        def line_flows(i, halves):
            a = i // TILES_PER_AREA
            run = min(a, len(flow_runs) - 1)
            if i not in flow:
                if i == TILES - 1:
                    flow[i] = psum.tile([P, L], F32, name="last_flow", tag="current00")
                else:
                    flow[i] = psum.tile([P, L], F32, name="flow", tag="flow", bufs=2)
            for g in halves:
                codes, scales = power_q[i, g]
                nc.tensor.matmul_mx(
                    out=flow[i][:],
                    lhsT=codes.bitcast(FP8X4),
                    lhsT_scale=scales,
                    rhs=flow_factor[a][:, g, :].bitcast(FP4X4),
                    rhs_scale=flow_scales[run][:, 2 * (a - flow_runs[run][0]) + g, :],
                    start=(g == 0),
                    stop=(g == 1),
                )

        def store(i, copy):
            result = keep.tile([P, L], F32, name="result%d" % i)
            copy(out=result[:], in_=flow[i][:])
            nc.sync.dma_start(out=tile_rows(out, i), in_=result[:])

        def src_due(step):
            return [step + 2, step + 3] if step % 2 == 0 and step + 2 < TILES else []

        def step_keys(step):
            i = step - 2
            keys = []
            if i >= 0:
                keys.extend([("sum", i, 1), ("power", i, 1)] if i % 2 == 1 else [("power", i, 2)])
            if src_due(step):
                keys.append(("src", src_due(step)[0], 2))
            return keys

        def step_operands(step):
            operands = [(power_q, (step - 2, g)) for g in both] if step >= 2 else []
            return operands + [(src_q, i) for i in src_due(step)]

        both = (0, 1)
        last = TILES - 1

        for i in range(2):
            turn_src_as_loaded([i])
        for i in range(2):
            stage(("head", i), [("src", i, 1)], ("src", i, 1))
            quantize(("head", i), [(src_q, i)])
        for c, g in parts:
            currents(0, c, g)
        turn_src_as_loaded(src_due(0))
        stage(0, step_keys(0), ("src", 2, 2))

        for step in range(TILES):
            even = step % 2 == 0
            if step >= 2:
                stage(step, step_keys(step), ("power", step - 2, 2 if even else 1))
            if even and step >= 2:
                stage(step + 1, step_keys(step + 1), ("sum", step - 1, 1))
            if not even and src_due(step + 1):
                stage(step + 1, step_keys(step + 1), ("src", src_due(step + 1)[0], 2))
            if src_due(step + 2):
                sort_src(src_due(step + 2))
            for n, (c, g) in enumerate(parts[:3]):
                multiply(step, c, g)
                if n == 1 and step >= 3:
                    line_flows(step - 3, both)
                    store(step - 3, nc.scalar.copy)
                if step < last:
                    currents(step + 1, c, g)
            if even:
                add_products(step, nc.gpsimd, 0, EARLY_SUM)
            if step == last:
                turn_and_add(step)
            if step >= 1:
                turn_power(step - 1, (1,) if even else both)
            if src_due(step + 2):
                turn_sorted_src(src_due(step + 2))
            if step < last:
                if not even:
                    turn_and_add(step)
                multiply(step, 1, 1, 0, P - GATE)
                if step_keys(step):
                    quantize(step, step_operands(step))
                multiply(step, 1, 1, P - GATE, P)
                currents(step + 1, 1, 1)
                add_products(step, nc.gpsimd, EARLY_SUM if even else HALF, N)
            else:
                multiply(step, 1, 1)
                quantize(step, step_operands(step))

        stage(("last", 0), [("sum", last, 1)], ("sum", last, 1))
        stage(TILES, step_keys(TILES), ("power", last - 1, 2))
        line_flows(last - 2, both)
        add_products(last, nc.vector, HALF, N)
        turn_power(last, (1,))
        quantize(TILES, step_operands(TILES))
        line_flows(last - 1, both)
        quantize(("last", 0), [(power_q, (last, 0))])
        line_flows(last, (0,))
        stage(("last", 1), [("power", last, 1)], ("power", last, 1))
        store(last - 2, nc.scalar.copy)
        quantize(("last", 1), [(power_q, (last, 1))])
        line_flows(last, (1,))
        store(last - 1, nc.vector.tensor_copy)
        store(last, nc.scalar.copy)
